import numpy as np
import ml_dtypes


def mxq(x, axis, fmt="e4m3"):
    dtype, down = {"e4m3": (ml_dtypes.float8_e4m3fn, 7), "e5m2": (ml_dtypes.float8_e5m2, 14)}[fmt]
    v = np.moveaxis(np.asarray(x, np.float32).astype(ml_dtypes.bfloat16).astype(np.float64), axis, -1)
    blocks = v.reshape(v.shape[:-1] + (-1, 32))
    amax = np.abs(blocks).max(-1, keepdims=True)
    byte = np.maximum(np.where(amax > 0, np.frexp(amax)[1] - 1 + 127, 0) - down, 1)
    scale = np.exp2(byte - 127.0)
    codes = (blocks / scale).astype(np.float32).astype(dtype).astype(np.float64)
    return np.moveaxis((codes * scale).reshape(v.shape), -1, axis)


WIDE = False


def mx_kscale(k):
    if not WIDE:
        return np.ones(k)
    levels = np.array([10, -10, 5, -5, 0])
    if k % 512:
        return np.exp2(np.random.permutation(np.resize(levels, k // 32))).repeat(32)
    a = np.empty((k // 512, 16))
    for p in range(k // 512):
        a[p, :8] = np.random.permutation(np.resize(levels, 8))
        for g in range(8):
            far = levels[np.abs(levels - a[p, g]) >= 10]
            a[p, g + 8] = far[np.random.randint(len(far))]
    return np.exp2(a.ravel()).repeat(32)


def f64(x):
    return np.asarray(x).astype(np.float64)


def striped(idx):
    return np.tile(idx.reshape(-1, 16).T, (8, 1)).astype(np.uint16)


def unstriped(offs):
    return offs[:16].T.reshape(-1).astype(np.int64)


def silu(v):
    return v / (1.0 + np.exp(-np.maximum(v, -700.0)))


K, T, E, C, H, N = 2560, 768, 4, 128, 512, 512


def by_expert(wq, xq):
    return np.concatenate([wq[e].T @ xq[:, e * C:(e + 1) * C] for e in range(E)], axis=1)


def setup_inputs():
    n = np.random.standard_normal
    s = mx_kscale(K)[:, None]
    u = mx_kscale(H)
    return {
        "xT": (n((K, T)) * s).astype(np.float32),
        "w1": (n((E, K, H)) / np.sqrt(K) / s[None] * u[None, None, :]).astype(np.float32),
        "w2": (n((E, H, N)) / np.sqrt(H) / u[None, :, None]).astype(np.float32),
        "gate": np.tile(np.random.uniform(0.2, 1.0, E * C), (N, 1)).astype(np.float32),
        "offs": striped(np.random.permutation(T)[:E * C]),
    }


def reference(xT, w1, w2, gate, offs):
    idx = unstriped(offs)
    xq = mxq(f64(xT)[:, idx], 0, "e4m3")
    h = silu(by_expert(mxq(f64(w1), 1, "e4m3"), xq))
    y = by_expert(mxq(f64(w2), 1, "e4m3"), mxq(h, 0, "e4m3"))
    out = np.zeros((N, T))
    out[:, idx] = f64(gate) * y
    return out

@@ -1,0 +1,161 @@
+from contextlib import ExitStack
+
+import concourse.mybir as mybir
+
+K, T, E, C, H, N = 2560, 768, 4, 128, 512, 512
+SLOTS = E * C
+
+FLOPS = 2 * SLOTS * (K * H + H * N)
+BYTES = 4 * (K * T + E * K * H + E * H * N + SLOTS + N * T) + 2 * 128 * (SLOTS // 16)
+
+F32 = mybir.dt.float32
+BF16 = mybir.dt.bfloat16
+U32 = mybir.dt.uint32
+U16 = mybir.dt.uint16
+U8 = mybir.dt.uint8
+FP8X4 = mybir.dt.float8_e4m3fn_x4
+
+P = 128
+PACK = 4
+PASSES = K // (P * PACK)
+VECTOR_CHUNKS = {(0, 2), (0, 5), (1, 2), (1, 5), (2, 2), (2, 5), (3, 1)}
+
+
+def tile_routed_moe_kernel(tc, xT, w1, w2, gate, offs, out):
+    nc = tc.nc
+    mult = mybir.AluOpType.mult
+    silu = mybir.ActivationFunctionType.Silu
+
+    x_rows = xT.rearrange("(g p u e) t -> g u p e t", g=PASSES, u=2, e=2)
+    w1_rows = w1.rearrange("e (g p j) c -> e g p j c", g=PASSES, j=PACK)
+    w2_rows = w2.rearrange("e (p j) c -> e p j c", j=PACK)
+
+    with ExitStack() as ctx:
+        keep = ctx.enter_context(tc.tile_pool(name="keep", bufs=1))
+        x_stage = ctx.enter_context(tc.tile_pool(name="x_stage", bufs=4))
+        w_stage = ctx.enter_context(tc.tile_pool(name="w_stage", bufs=8))
+        w_group = ctx.enter_context(tc.tile_pool(name="w_group", bufs=4))
+        w_quant = ctx.enter_context(tc.tile_pool(name="w_quant", bufs=12))
+        x_quant = ctx.enter_context(tc.tile_pool(name="x_quant", bufs=PASSES))
+        small = ctx.enter_context(tc.tile_pool(name="small", bufs=2))
+        last_psum = ctx.enter_context(tc.psum_pool(name="last_psum", bufs=1))
+        psum = ctx.enter_context(tc.psum_pool(name="psum", bufs=2))
+
+        offsets = keep.tile([P, SLOTS // 16], U16)
+        nc.sync.dma_start(offsets[:], offs)
+
+        windows = []
+        for b in range(N // P):
+            window = keep.tile([P, T], F32, name=f"window{b}")
+            nc.vector.memset(window[:], 0.0)
+            windows.append(window)
+
+        def dispatch(g):
+            slots = x_stage.tile([P, SLOTS * PACK], BF16, align_bytes=64)
+            words = slots[:].bitcast(U32).rearrange("p (n u) -> p n u", u=2)
+            for u in range(2):
+                x_raw = x_stage.tile([P, 2, T], F32)
+                nc.sync.dma_start(out=x_raw[:], in_=x_rows[g, u])
+                pairs = x_stage.tile([P, 2 * T], BF16, align_bytes=64)
+                nc.scalar.copy(
+                    out=pairs[:].rearrange("p (c i e) -> p c e i", i=4, e=2),
+                    in_=x_raw[:].rearrange("p e (c i) -> p c e i", i=4),
+                )
+                nc.vector.tensor_copy(words[:, :, u], pairs[:].bitcast(U32).indirect(offsets[:]))
+            x_codes = x_quant.tile([P, SLOTS], U32, align_bytes=64)
+            x_scales = x_quant.tile([P, SLOTS], U8, align_bytes=64)
+            nc.vector.quantize_mx(out=x_codes[:].bitcast(FP8X4), scales=x_scales[:], in_=slots[:])
+            return x_codes, x_scales
+
+        def share_of(e, g):
+            if e == E - 1 and g >= PASSES - 1:
+                return 48
+            return 0 if (e, g) in VECTOR_CHUNKS else 128
+
+        def weights(rows, permuted, share):
+            w_raw = w_stage.tile([P, PACK, 512], F32)
+            nc.sync.dma_start(out=w_raw[:], in_=rows)
+            grouped = w_group.tile([P, 2048], BF16, align_bytes=64)
+            if permuted:
+                dst = grouped[:].rearrange("p (t m j) -> p m j t", t=4, j=4)
+                src = w_raw[:].rearrange("p j (m t) -> p m j t", t=4)
+            else:
+                dst = grouped[:].rearrange("p (m t j) -> p m j t", t=4, j=4)
+                src = w_raw[:].rearrange("p j (m t) -> p m j t", t=4)
+            if share > 0:
+                nc.scalar.copy(out=dst[:, :share], in_=src[:, :share])
+            if share < 128:
+                nc.vector.tensor_copy(out=dst[:, share:], in_=src[:, share:])
+            w_codes = w_quant.tile([P, 512], U32, align_bytes=64)
+            w_scales = w_quant.tile([P, 512], U8, align_bytes=64)
+            nc.vector.quantize_mx(out=w_codes[:].bitcast(FP8X4), scales=w_scales[:], in_=grouped[:])
+            return w_codes, w_scales
+
+        def multiply(acc, w, cols_w, x, cols_x, start, stop):
+            nc.tensor.matmul_mx(
+                out=acc,
+                lhsT=w[0][:, cols_w].bitcast(FP8X4),
+                lhsT_scale=w[1][:, cols_w],
+                rhs=x[0][:, cols_x].bitcast(FP8X4),
+                rhs_scale=x[1][:, cols_x],
+                start=start,
+                stop=stop,
+            )
+
+        tokens = []
+        for e in range(E):
+            w1_q = []
+            for g in range(PASSES):
+                if e == 0:
+                    tokens.append(dispatch(g))
+                w1_q.append(weights(w1_rows[e, g], True, share_of(e, g)))
+            if e == 0:
+                gates = keep.tile([P, SLOTS], F32)
+                nc.sync.dma_start(out=gates[:], in_=gate[0:P, :])
+            w2_q = weights(w2_rows[e], False, share_of(e, PASSES))
+            mine = slice(e * C, (e + 1) * C)
+
+            h_grouped = small.tile([P, C * 4], BF16, align_bytes=64)
+            if e < E - 1:
+                hidden = psum.tile([P, 4, C], F32)
+                for t in range(4):
+                    for g in range(PASSES):
+                        multiply(hidden[:, t, :], w1_q[g], slice(t * P, (t + 1) * P), tokens[g], mine, g == 0, g == PASSES - 1)
+                nc.scalar.activation(
+                    out=h_grouped[:].rearrange("p (n t) -> p n t", t=4),
+                    in_=hidden[:].rearrange("p t n -> p n t"),
+                    func=silu,
+                )
+            else:
+                banks = []
+                for t in range(4):
+                    bank = last_psum.tile([P, C], F32, name=f"bank{t}")
+                    banks.append(bank)
+                for g in range(PASSES):
+                    for t in range(4):
+                        multiply(banks[t][:], w1_q[g], slice(t * P, (t + 1) * P), tokens[g], mine, g == 0, g == PASSES - 1)
+                for t in range(4):
+                    nc.scalar.activation(
+                        out=h_grouped[:].rearrange("p (n t) -> p n t", t=4)[:, :, t],
+                        in_=banks[t][:],
+                        func=silu,
+                    )
+            h_codes = small.tile([P, C], U32, align_bytes=64)
+            h_scales = small.tile([P, C], U8, align_bytes=64)
+            nc.vector.quantize_mx(out=h_codes[:].bitcast(FP8X4), scales=h_scales[:], in_=h_grouped[:])
+
+            product = psum.tile([P, 4, C], F32)
+            for b in range(4):
+                multiply(product[:, b, :], w2_q, slice(b * P, (b + 1) * P), (h_codes, h_scales), slice(0, C), True, True)
+            y = small.tile([P, 4, C], F32)
+            if e < E - 1:
+                nc.scalar.copy(out=y[:], in_=product[:])
+            for b in range(4):
+                if e == E - 1:
+                    nc.scalar.copy(out=y[:, b, :], in_=product[:, b, :])
+                nc.vector.tensor_tensor(
+                    windows[b][:].indirect(offsets[:, e * (C // 16) : (e + 1) * (C // 16)]), y[:, b, :], gates[:, mine], mult
+                )
+
+        for b in range(4):
+            nc.sync.dma_start(out=out[b * P : (b + 1) * P, :], in_=windows[b][:])

@@ -18,7 +18,7 @@ FP8X4 = mybir.dt.float8_e4m3fn_x4
 P = 128
 PACK = 4
 PASSES = K // (P * PACK)
-VECTOR_CHUNKS = {(0, 2), (0, 5), (1, 2), (1, 5), (2, 2), (2, 5), (3, 1)}
+VECTOR_CHUNKS = {(0, 2), (0, 5), (1, 2), (1, 5), (2, 2), (3, 1)}
 
 
 def tile_routed_moe_kernel(tc, xT, w1, w2, gate, offs, out):
@@ -91,6 +91,19 @@ def tile_routed_moe_kernel(tc, xT, w1, w2, gate, offs, out):
             nc.vector.quantize_mx(out=w_codes[:].bitcast(FP8X4), scales=w_scales[:], in_=grouped[:])
             return w_codes, w_scales
 
+        def half_of_last(h):
+            l_raw = small.tile([P, PACK, 256], F32)
+            nc.sync.dma_start(out=l_raw[:], in_=w2_rows[E - 1][:, :, h * 256 : (h + 1) * 256])
+            l_grouped = small.tile([P, 1024], BF16, align_bytes=64)
+            dst = l_grouped[:].rearrange("p (m t j) -> p m j t", t=4, j=4)
+            src = l_raw[:].rearrange("p j (m t) -> p m j t", t=4)
+            nc.scalar.copy(out=dst[:, :24], in_=src[:, :24])
+            nc.vector.tensor_copy(out=dst[:, 24:], in_=src[:, 24:])
+            l_codes = small.tile([P, 256], U32, align_bytes=64)
+            l_scales = small.tile([P, 256], U8, align_bytes=64)
+            nc.vector.quantize_mx(out=l_codes[:].bitcast(FP8X4), scales=l_scales[:], in_=l_grouped[:])
+            return l_codes, l_scales
+
         def multiply(acc, w, cols_w, x, cols_x, start, stop):
             nc.tensor.matmul_mx(
                 out=acc,
@@ -112,7 +125,12 @@ def tile_routed_moe_kernel(tc, xT, w1, w2, gate, offs, out):
             if e == 0:
                 gates = keep.tile([P, SLOTS], F32)
                 nc.sync.dma_start(out=gates[:], in_=gate[0:P, :])
-            w2_q = weights(w2_rows[e], False, share_of(e, PASSES))
+            if e < E - 1:
+                whole = weights(w2_rows[e], False, share_of(e, PASSES))
+                w2_q = [(whole, b * P) for b in range(4)]
+            else:
+                halves = [half_of_last(h) for h in range(2)]
+                w2_q = [(halves[b // 2], (b % 2) * P) for b in range(4)]
             mine = slice(e * C, (e + 1) * C)
 
             h_grouped = small.tile([P, C * 4], BF16, align_bytes=64)
@@ -146,16 +164,16 @@ def tile_routed_moe_kernel(tc, xT, w1, w2, gate, offs, out):
 
             product = psum.tile([P, 4, C], F32)
             for b in range(4):
-                multiply(product[:, b, :], w2_q, slice(b * P, (b + 1) * P), (h_codes, h_scales), slice(0, C), True, True)
+                multiply(product[:, b, :], w2_q[b][0], slice(w2_q[b][1], w2_q[b][1] + P), (h_codes, h_scales), slice(0, C), True, True)
             y = small.tile([P, 4, C], F32)
+            weight = gates[:, mine].unsqueeze(1)
             if e < E - 1:
-                nc.scalar.copy(out=y[:], in_=product[:])
+                nc.vector.tensor_tensor(y[:], product[:], weight.to_broadcast([P, 4, C]), mult)
+            else:
+                for b in range(0, 4, 2):
+                    nc.vector.tensor_tensor(y[:, b : b + 2, :], product[:, b : b + 2, :], weight.to_broadcast([P, 2, C]), mult)
             for b in range(4):
-                if e == E - 1:
-                    nc.scalar.copy(out=y[:, b, :], in_=product[:, b, :])
-                nc.vector.tensor_tensor(
-                    windows[b][:].indirect(offsets[:, e * (C // 16) : (e + 1) * (C // 16)]), y[:, b, :], gates[:, mine], mult
-                )
+                nc.vector.tensor_copy(windows[b][:].indirect(offsets[:, e * (C // 16) : (e + 1) * (C // 16)]), y[:, b, :])
 
         for b in range(4):
             nc.sync.dma_start(out=out[b * P : (b + 1) * P, :], in_=windows[b][:])

@@ -19,6 +19,8 @@ P = 128
 PACK = 4
 PASSES = K // (P * PACK)
 VECTOR_CHUNKS = {(0, 2), (0, 5), (1, 2), (1, 5), (2, 2), (3, 1)}
+LATE = []
+PAIRED = {(1, 0), (1, 2), (2, 0), (2, 2)}
 
 
 def tile_routed_moe_kernel(tc, xT, w1, w2, gate, offs, out):
@@ -28,16 +30,19 @@ def tile_routed_moe_kernel(tc, xT, w1, w2, gate, offs, out):
 
     x_rows = xT.rearrange("(g p u e) t -> g u p e t", g=PASSES, u=2, e=2)
     w1_rows = w1.rearrange("e (g p j) c -> e g p j c", g=PASSES, j=PACK)
+    w1_pairs = w1.rearrange("e (g p j) c -> e p g j c", g=PASSES, j=PACK)
     w2_rows = w2.rearrange("e (p j) c -> e p j c", j=PACK)
 
     with ExitStack() as ctx:
         keep = ctx.enter_context(tc.tile_pool(name="keep", bufs=1))
         x_stage = ctx.enter_context(tc.tile_pool(name="x_stage", bufs=4))
-        w_stage = ctx.enter_context(tc.tile_pool(name="w_stage", bufs=8))
+        w_stage = ctx.enter_context(tc.tile_pool(name="w_stage", bufs=5))
+        p_stage = ctx.enter_context(tc.tile_pool(name="p_stage", bufs=2))
         w_group = ctx.enter_context(tc.tile_pool(name="w_group", bufs=4))
-        w_quant = ctx.enter_context(tc.tile_pool(name="w_quant", bufs=12))
+        w_quant = ctx.enter_context(tc.tile_pool(name="w_quant", bufs=8))
         x_quant = ctx.enter_context(tc.tile_pool(name="x_quant", bufs=PASSES))
-        small = ctx.enter_context(tc.tile_pool(name="small", bufs=2))
+        small = ctx.enter_context(tc.tile_pool(name="small", bufs=4))
+        halves_pool = ctx.enter_context(tc.tile_pool(name="halves", bufs=2))
         last_psum = ctx.enter_context(tc.psum_pool(name="last_psum", bufs=1))
         psum = ctx.enter_context(tc.psum_pool(name="psum", bufs=2))
 
@@ -67,41 +72,62 @@ def tile_routed_moe_kernel(tc, xT, w1, w2, gate, offs, out):
             nc.vector.quantize_mx(out=x_codes[:].bitcast(FP8X4), scales=x_scales[:], in_=slots[:])
             return x_codes, x_scales
 
-        def share_of(e, g):
-            if e == E - 1 and g >= PASSES - 1:
-                return 48
-            return 0 if (e, g) in VECTOR_CHUNKS else 128
-
-        def weights(rows, permuted, share):
-            w_raw = w_stage.tile([P, PACK, 512], F32)
-            nc.sync.dma_start(out=w_raw[:], in_=rows)
-            grouped = w_group.tile([P, 2048], BF16, align_bytes=64)
-            if permuted:
-                dst = grouped[:].rearrange("p (t m j) -> p m j t", t=4, j=4)
-                src = w_raw[:].rearrange("p j (m t) -> p m j t", t=4)
+        def interleave(grouped, raw, permuted, on_vector, lo=0, hi=128):
+            order = "p (t m j) -> p m j t" if permuted else "p (m t j) -> p m j t"
+            dst = grouped.rearrange(order, t=4, j=4)[:, lo:hi]
+            src = raw.rearrange("p j (m t) -> p m j t", t=4)[:, lo:hi]
+            if on_vector:
+                nc.vector.tensor_copy(out=dst, in_=src)
             else:
-                dst = grouped[:].rearrange("p (m t j) -> p m j t", t=4, j=4)
-                src = w_raw[:].rearrange("p j (m t) -> p m j t", t=4)
-            if share > 0:
-                nc.scalar.copy(out=dst[:, :share], in_=src[:, :share])
-            if share < 128:
-                nc.vector.tensor_copy(out=dst[:, share:], in_=src[:, share:])
+                nc.scalar.copy(out=dst, in_=src)
+
+        def quantised(grouped):
             w_codes = w_quant.tile([P, 512], U32, align_bytes=64)
             w_scales = w_quant.tile([P, 512], U8, align_bytes=64)
             nc.vector.quantize_mx(out=w_codes[:].bitcast(FP8X4), scales=w_scales[:], in_=grouped[:])
             return w_codes, w_scales
 
-        def half_of_last(h):
-            l_raw = small.tile([P, PACK, 256], F32)
-            nc.sync.dma_start(out=l_raw[:], in_=w2_rows[E - 1][:, :, h * 256 : (h + 1) * 256])
-            l_grouped = small.tile([P, 1024], BF16, align_bytes=64)
-            dst = l_grouped[:].rearrange("p (m t j) -> p m j t", t=4, j=4)
-            src = l_raw[:].rearrange("p j (m t) -> p m j t", t=4)
-            nc.scalar.copy(out=dst[:, :24], in_=src[:, :24])
-            nc.vector.tensor_copy(out=dst[:, 24:], in_=src[:, 24:])
+        def weights(raw, permuted, on_vector):
+            grouped = w_group.tile([P, 2048], BF16, align_bytes=64)
+            interleave(grouped[:], raw, permuted, on_vector)
+            return quantised(grouped)
+
+        def loaded(rows):
+            w_raw = w_stage.tile([P, PACK, 512], F32)
+            nc.sync.dma_start(out=w_raw[:], in_=rows)
+            return w_raw[:]
+
+        def loaded_pair(e, g):
+            p_raw = p_stage.tile([P, 2, PACK, 512], F32)
+            nc.sync.dma_start(out=p_raw[:], in_=w1_pairs[e][:, g : g + 2])
+            return [p_raw[:, 0], p_raw[:, 1]]
+
+        def last_of_w1():
+            w_raw = w_stage.tile([P, PACK, 512], F32)
+            grouped = w_group.tile([P, 2048], BF16, align_bytes=64)
+            for h in range(2):
+                half = slice(h * 256, (h + 1) * 256)
+                nc.sync.dma_start(out=w_raw[:, :, half], in_=w1_rows[E - 1, PASSES - 1][:, :, half])
+            for on_vector, lo, hi in ((False, 0, 40), (True, 40, 64), (False, 64, 84), (True, 84, 128)):
+                interleave(grouped[:], w_raw[:], True, on_vector, lo, hi)
+            quarters = []
+            for h in range(2):
+                l_codes = small.tile([P, 256], U32, align_bytes=64)
+                l_scales = small.tile([P, 256], U8, align_bytes=64)
+                nc.vector.quantize_mx(
+                    out=l_codes[:].bitcast(FP8X4), scales=l_scales[:], in_=grouped[:, h * 1024 : (h + 1) * 1024]
+                )
+                quarters.append((l_codes, l_scales))
+            return quarters
+
+        def half_of_w2(e, h, on_vector):
+            h_raw = halves_pool.tile([P, PACK, 256], F32)
+            nc.sync.dma_start(out=h_raw[:], in_=w2_rows[e][:, :, h * 256 : (h + 1) * 256])
+            h_rows = halves_pool.tile([P, 1024], BF16, align_bytes=64)
+            interleave(h_rows[:], h_raw[:], False, on_vector, 0, 64)
             l_codes = small.tile([P, 256], U32, align_bytes=64)
             l_scales = small.tile([P, 256], U8, align_bytes=64)
-            nc.vector.quantize_mx(out=l_codes[:].bitcast(FP8X4), scales=l_scales[:], in_=l_grouped[:])
+            nc.vector.quantize_mx(out=l_codes[:].bitcast(FP8X4), scales=l_scales[:], in_=h_rows[:])
             return l_codes, l_scales
 
         def multiply(acc, w, cols_w, x, cols_x, start, stop):
@@ -115,35 +141,19 @@ def tile_routed_moe_kernel(tc, xT, w1, w2, gate, offs, out):
                 stop=stop,
             )
 
-        tokens = []
-        for e in range(E):
-            w1_q = []
-            for g in range(PASSES):
-                if e == 0:
-                    tokens.append(dispatch(g))
-                w1_q.append(weights(w1_rows[e, g], True, share_of(e, g)))
-            if e == 0:
-                gates = keep.tile([P, SLOTS], F32)
-                nc.sync.dma_start(out=gates[:], in_=gate[0:P, :])
-            if e < E - 1:
-                whole = weights(w2_rows[e], False, share_of(e, PASSES))
-                w2_q = [(whole, b * P) for b in range(4)]
-            else:
-                halves = [half_of_last(h) for h in range(2)]
-                w2_q = [(halves[b // 2], (b % 2) * P) for b in range(4)]
-            mine = slice(e * C, (e + 1) * C)
+        def scatter(e, b, y):
+            nc.vector.tensor_copy(windows[b][:].indirect(offsets[:, e * (C // 16) : (e + 1) * (C // 16)]), y)
 
+        def first_layer(e, w1_q):
+            mine = slice(e * C, (e + 1) * C)
             h_grouped = small.tile([P, C * 4], BF16, align_bytes=64)
+            h_view = h_grouped[:].rearrange("p (n t) -> p n t", t=4)
             if e < E - 1:
                 hidden = psum.tile([P, 4, C], F32)
                 for t in range(4):
                     for g in range(PASSES):
                         multiply(hidden[:, t, :], w1_q[g], slice(t * P, (t + 1) * P), tokens[g], mine, g == 0, g == PASSES - 1)
-                nc.scalar.activation(
-                    out=h_grouped[:].rearrange("p (n t) -> p n t", t=4),
-                    in_=hidden[:].rearrange("p t n -> p n t"),
-                    func=silu,
-                )
+                nc.scalar.activation(out=h_view, in_=hidden[:].rearrange("p t n -> p n t"), func=silu)
             else:
                 banks = []
                 for t in range(4):
@@ -151,29 +161,75 @@ def tile_routed_moe_kernel(tc, xT, w1, w2, gate, offs, out):
                     banks.append(bank)
                 for g in range(PASSES):
                     for t in range(4):
-                        multiply(banks[t][:], w1_q[g], slice(t * P, (t + 1) * P), tokens[g], mine, g == 0, g == PASSES - 1)
+                        codes, first = (w1_q[g], t * P) if g < PASSES - 1 else (w1_q[g][t // 2], t % 2 * P)
+                        multiply(banks[t][:], codes, slice(first, first + P), tokens[g], mine, g == 0, g == PASSES - 1)
                 for t in range(4):
-                    nc.scalar.activation(
-                        out=h_grouped[:].rearrange("p (n t) -> p n t", t=4)[:, :, t],
-                        in_=banks[t][:],
-                        func=silu,
-                    )
+                    nc.scalar.activation(out=h_view[:, :, t], in_=banks[t][:], func=silu)
             h_codes = small.tile([P, C], U32, align_bytes=64)
             h_scales = small.tile([P, C], U8, align_bytes=64)
             nc.vector.quantize_mx(out=h_codes[:].bitcast(FP8X4), scales=h_scales[:], in_=h_grouped[:])
+            return h_codes, h_scales
 
+        def second_layer(e, h_q, w2_q, blocks):
+            n = len(blocks)
             product = psum.tile([P, 4, C], F32)
-            for b in range(4):
-                multiply(product[:, b, :], w2_q[b][0], slice(w2_q[b][1], w2_q[b][1] + P), (h_codes, h_scales), slice(0, C), True, True)
+            for i in range(n):
+                multiply(product[:, i, :], w2_q, slice(i * P, (i + 1) * P), h_q, slice(0, C), True, True)
             y = small.tile([P, 4, C], F32)
-            weight = gates[:, mine].unsqueeze(1)
-            if e < E - 1:
-                nc.vector.tensor_tensor(y[:], product[:], weight.to_broadcast([P, 4, C]), mult)
+            weight = gates[:, e * C : (e + 1) * C].unsqueeze(1)
+            nc.vector.tensor_tensor(y[:, :n, :], product[:, :n, :], weight.to_broadcast([P, n, C]), mult)
+            return [(e, b, y[:, i, :]) for i, b in enumerate(blocks)]
+
+        tokens = []
+        hidden_q = []
+        waiting = []
+        late = []
+        for e in range(E):
+            w1_q = []
+            raws = {}
+            for g in range(PASSES):
+                if e == 0:
+                    tokens.append(dispatch(g))
+                if e == E - 1 and g == PASSES - 1:
+                    w1_q.append(last_of_w1())
+                else:
+                    if (e, g) in PAIRED:
+                        raws[g], raws[g + 1] = loaded_pair(e, g)
+                    elif g not in raws:
+                        raws[g] = loaded(w1_rows[e, g])
+                    w1_q.append(weights(raws[g], True, (e, g) in VECTOR_CHUNKS))
+                if g >= 0 and waiting:
+                    scatter(*waiting.pop(0))
+            while waiting:
+                scatter(*waiting.pop(0))
+            if e == 0:
+                gates = keep.tile([P, SLOTS], F32)
+                ones = keep.tile([P, P], F32)
+                nc.vector.memset(ones[:], 1.0)
+                row = keep.tile([P, SLOTS], F32)
+                nc.vector.memset(row[:], 0.0)
+                nc.sync.dma_start(out=row[0:1, :], in_=gate[0:1, :])
+                product = psum.tile([P, 4, C], F32)
+                nc.tensor.matmul(product[:].rearrange("p b n -> p (b n)"), ones[:], row[:], start=True, stop=True)
+                nc.scalar.copy(out=gates[:], in_=product[:].rearrange("p b n -> p (b n)"))
+            if e in LATE:
+                w2_q = half_of_w2(e, 0, (e, PASSES) in VECTOR_CHUNKS)
+                hidden_q.append(first_layer(e, w1_q))
+                waiting = second_layer(e, hidden_q[e], w2_q, [0, 1])
+            elif e < E - 1:
+                w2_q = weights(loaded(w2_rows[e]), False, (e, PASSES) in VECTOR_CHUNKS)
+                hidden_q.append(first_layer(e, w1_q))
+                waiting = second_layer(e, hidden_q[e], w2_q, [0, 1, 2, 3])
             else:
-                for b in range(0, 4, 2):
-                    nc.vector.tensor_tensor(y[:, b : b + 2, :], product[:, b : b + 2, :], weight.to_broadcast([P, 2, C]), mult)
-            for b in range(4):
-                nc.vector.tensor_copy(windows[b][:].indirect(offsets[:, e * (C // 16) : (e + 1) * (C // 16)]), y[:, b, :])
+                late = [half_of_w2(f, 1, False) for f in LATE]
+                w2_q = [half_of_w2(e, h, h == 1) for h in range(2)]
+                hidden_q.append(first_layer(e, w1_q))
+        for f, w2_late in zip(LATE, late):
+            for args in second_layer(f, hidden_q[f], w2_late, [2, 3]):
+                scatter(*args)
+        for h in range(2):
+            for args in second_layer(E - 1, hidden_q[E - 1], w2_q[h], [2 * h, 2 * h + 1]):
+                scatter(*args)
 
         for b in range(4):
             nc.sync.dma_start(out=out[b * P : (b + 1) * P, :], in_=windows[b][:])

from contextlib import ExitStack

import concourse.mybir as mybir

K, T, E, C, H, N = 2560, 768, 4, 128, 512, 512
SLOTS = E * C

FLOPS = 2 * SLOTS * (K * H + H * N)
BYTES = 4 * (K * T + E * K * H + E * H * N + SLOTS + N * T) + 2 * 128 * (SLOTS // 16)

F32 = mybir.dt.float32
BF16 = mybir.dt.bfloat16
U32 = mybir.dt.uint32
U16 = mybir.dt.uint16
U8 = mybir.dt.uint8
FP8X4 = mybir.dt.float8_e4m3fn_x4

P = 128
PACK = 4
PASSES = K // (P * PACK)
VECTOR_CHUNKS = {(0, 2), (0, 5), (1, 2), (1, 5), (2, 2), (3, 1)}
LATE = []
PAIRED = {(1, 0), (1, 2), (2, 0), (2, 2)}


def tile_routed_moe_kernel(tc, xT, w1, w2, gate, offs, out):
    nc = tc.nc
    mult = mybir.AluOpType.mult
    silu = mybir.ActivationFunctionType.Silu

    x_rows = xT.rearrange("(g p u e) t -> g u p e t", g=PASSES, u=2, e=2)
    w1_rows = w1.rearrange("e (g p j) c -> e g p j c", g=PASSES, j=PACK)
    w1_pairs = w1.rearrange("e (g p j) c -> e p g j c", g=PASSES, j=PACK)
    w2_rows = w2.rearrange("e (p j) c -> e p j c", j=PACK)

    with ExitStack() as ctx:
        keep = ctx.enter_context(tc.tile_pool(name="keep", bufs=1))
        x_stage = ctx.enter_context(tc.tile_pool(name="x_stage", bufs=4))
        w_stage = ctx.enter_context(tc.tile_pool(name="w_stage", bufs=5))
        p_stage = ctx.enter_context(tc.tile_pool(name="p_stage", bufs=2))
        w_group = ctx.enter_context(tc.tile_pool(name="w_group", bufs=4))
        w_quant = ctx.enter_context(tc.tile_pool(name="w_quant", bufs=8))
        x_quant = ctx.enter_context(tc.tile_pool(name="x_quant", bufs=PASSES))
        small = ctx.enter_context(tc.tile_pool(name="small", bufs=4))
        halves_pool = ctx.enter_context(tc.tile_pool(name="halves", bufs=2))
        last_psum = ctx.enter_context(tc.psum_pool(name="last_psum", bufs=1))
        psum = ctx.enter_context(tc.psum_pool(name="psum", bufs=2))

        offsets = keep.tile([P, SLOTS // 16], U16)
        nc.sync.dma_start(offsets[:], offs)

        windows = []
        for b in range(N // P):
            window = keep.tile([P, T], F32, name=f"window{b}")
            nc.vector.memset(window[:], 0.0)
            windows.append(window)

        def dispatch(g):
            slots = x_stage.tile([P, SLOTS * PACK], BF16, align_bytes=64)
            words = slots[:].bitcast(U32).rearrange("p (n u) -> p n u", u=2)
            for u in range(2):
                x_raw = x_stage.tile([P, 2, T], F32)
                nc.sync.dma_start(out=x_raw[:], in_=x_rows[g, u])
                pairs = x_stage.tile([P, 2 * T], BF16, align_bytes=64)
                nc.scalar.copy(
                    out=pairs[:].rearrange("p (c i e) -> p c e i", i=4, e=2),
                    in_=x_raw[:].rearrange("p e (c i) -> p c e i", i=4),
                )
                nc.vector.tensor_copy(words[:, :, u], pairs[:].bitcast(U32).indirect(offsets[:]))
            x_codes = x_quant.tile([P, SLOTS], U32, align_bytes=64)
            x_scales = x_quant.tile([P, SLOTS], U8, align_bytes=64)
            nc.vector.quantize_mx(out=x_codes[:].bitcast(FP8X4), scales=x_scales[:], in_=slots[:])
            return x_codes, x_scales

        def interleave(grouped, raw, permuted, on_vector, lo=0, hi=128):
            order = "p (t m j) -> p m j t" if permuted else "p (m t j) -> p m j t"
            dst = grouped.rearrange(order, t=4, j=4)[:, lo:hi]
            src = raw.rearrange("p j (m t) -> p m j t", t=4)[:, lo:hi]
            if on_vector:
                nc.vector.tensor_copy(out=dst, in_=src)
            else:
                nc.scalar.copy(out=dst, in_=src)

        def quantised(grouped):
            w_codes = w_quant.tile([P, 512], U32, align_bytes=64)
            w_scales = w_quant.tile([P, 512], U8, align_bytes=64)
            nc.vector.quantize_mx(out=w_codes[:].bitcast(FP8X4), scales=w_scales[:], in_=grouped[:])
            return w_codes, w_scales

        def weights(raw, permuted, on_vector):
            grouped = w_group.tile([P, 2048], BF16, align_bytes=64)
            interleave(grouped[:], raw, permuted, on_vector)
            return quantised(grouped)

        def loaded(rows):
            w_raw = w_stage.tile([P, PACK, 512], F32)
            nc.sync.dma_start(out=w_raw[:], in_=rows)
            return w_raw[:]

        def loaded_pair(e, g):
            p_raw = p_stage.tile([P, 2, PACK, 512], F32)
            nc.sync.dma_start(out=p_raw[:], in_=w1_pairs[e][:, g : g + 2])
            return [p_raw[:, 0], p_raw[:, 1]]

        def last_of_w1():
            w_raw = w_stage.tile([P, PACK, 512], F32)
            grouped = w_group.tile([P, 2048], BF16, align_bytes=64)
            for h in range(2):
                half = slice(h * 256, (h + 1) * 256)
                nc.sync.dma_start(out=w_raw[:, :, half], in_=w1_rows[E - 1, PASSES - 1][:, :, half])
            for on_vector, lo, hi in ((False, 0, 40), (True, 40, 64), (False, 64, 84), (True, 84, 128)):
                interleave(grouped[:], w_raw[:], True, on_vector, lo, hi)
            quarters = []
            for h in range(2):
                l_codes = small.tile([P, 256], U32, align_bytes=64)
                l_scales = small.tile([P, 256], U8, align_bytes=64)
                nc.vector.quantize_mx(
                    out=l_codes[:].bitcast(FP8X4), scales=l_scales[:], in_=grouped[:, h * 1024 : (h + 1) * 1024]
                )
                quarters.append((l_codes, l_scales))
            return quarters

        def half_of_w2(e, h, on_vector):
            h_raw = halves_pool.tile([P, PACK, 256], F32)
            nc.sync.dma_start(out=h_raw[:], in_=w2_rows[e][:, :, h * 256 : (h + 1) * 256])
            h_rows = halves_pool.tile([P, 1024], BF16, align_bytes=64)
            interleave(h_rows[:], h_raw[:], False, on_vector, 0, 64)
            l_codes = small.tile([P, 256], U32, align_bytes=64)
            l_scales = small.tile([P, 256], U8, align_bytes=64)
            nc.vector.quantize_mx(out=l_codes[:].bitcast(FP8X4), scales=l_scales[:], in_=h_rows[:])
            return l_codes, l_scales

        def multiply(acc, w, cols_w, x, cols_x, start, stop):
            nc.tensor.matmul_mx(
                out=acc,
                lhsT=w[0][:, cols_w].bitcast(FP8X4),
                lhsT_scale=w[1][:, cols_w],
                rhs=x[0][:, cols_x].bitcast(FP8X4),
                rhs_scale=x[1][:, cols_x],
                start=start,
                stop=stop,
            )

        def scatter(e, b, y):
            nc.vector.tensor_copy(windows[b][:].indirect(offsets[:, e * (C // 16) : (e + 1) * (C // 16)]), y)

        def first_layer(e, w1_q):
            mine = slice(e * C, (e + 1) * C)
            h_grouped = small.tile([P, C * 4], BF16, align_bytes=64)
            h_view = h_grouped[:].rearrange("p (n t) -> p n t", t=4)
            if e < E - 1:
                hidden = psum.tile([P, 4, C], F32)
                for t in range(4):
                    for g in range(PASSES):
                        multiply(hidden[:, t, :], w1_q[g], slice(t * P, (t + 1) * P), tokens[g], mine, g == 0, g == PASSES - 1)
                nc.scalar.activation(out=h_view, in_=hidden[:].rearrange("p t n -> p n t"), func=silu)
            else:
                banks = []
                for t in range(4):
                    bank = last_psum.tile([P, C], F32, name=f"bank{t}")
                    banks.append(bank)
                for g in range(PASSES):
                    for t in range(4):
                        codes, first = (w1_q[g], t * P) if g < PASSES - 1 else (w1_q[g][t // 2], t % 2 * P)
                        multiply(banks[t][:], codes, slice(first, first + P), tokens[g], mine, g == 0, g == PASSES - 1)
                for t in range(4):
                    nc.scalar.activation(out=h_view[:, :, t], in_=banks[t][:], func=silu)
            h_codes = small.tile([P, C], U32, align_bytes=64)
            h_scales = small.tile([P, C], U8, align_bytes=64)
            nc.vector.quantize_mx(out=h_codes[:].bitcast(FP8X4), scales=h_scales[:], in_=h_grouped[:])
            return h_codes, h_scales

        def second_layer(e, h_q, w2_q, blocks):
            n = len(blocks)
            product = psum.tile([P, 4, C], F32)
            for i in range(n):
                multiply(product[:, i, :], w2_q, slice(i * P, (i + 1) * P), h_q, slice(0, C), True, True)
            y = small.tile([P, 4, C], F32)
            weight = gates[:, e * C : (e + 1) * C].unsqueeze(1)
            nc.vector.tensor_tensor(y[:, :n, :], product[:, :n, :], weight.to_broadcast([P, n, C]), mult)
            return [(e, b, y[:, i, :]) for i, b in enumerate(blocks)]

        tokens = []
        hidden_q = []
        waiting = []
        late = []
        for e in range(E):
            w1_q = []
            raws = {}
            for g in range(PASSES):
                if e == 0:
                    tokens.append(dispatch(g))
                if e == E - 1 and g == PASSES - 1:
                    w1_q.append(last_of_w1())
                else:
                    if (e, g) in PAIRED:
                        raws[g], raws[g + 1] = loaded_pair(e, g)
                    elif g not in raws:
                        raws[g] = loaded(w1_rows[e, g])
                    w1_q.append(weights(raws[g], True, (e, g) in VECTOR_CHUNKS))
                if g >= 0 and waiting:
                    scatter(*waiting.pop(0))
            while waiting:
                scatter(*waiting.pop(0))
            if e == 0:
                gates = keep.tile([P, SLOTS], F32)
                ones = keep.tile([P, P], F32)
                nc.vector.memset(ones[:], 1.0)
                row = keep.tile([P, SLOTS], F32)
                nc.vector.memset(row[:], 0.0)
                nc.sync.dma_start(out=row[0:1, :], in_=gate[0:1, :])
                product = psum.tile([P, 4, C], F32)
                nc.tensor.matmul(product[:].rearrange("p b n -> p (b n)"), ones[:], row[:], start=True, stop=True)
                nc.scalar.copy(out=gates[:], in_=product[:].rearrange("p b n -> p (b n)"))
            if e in LATE:
                w2_q = half_of_w2(e, 0, (e, PASSES) in VECTOR_CHUNKS)
                hidden_q.append(first_layer(e, w1_q))
                waiting = second_layer(e, hidden_q[e], w2_q, [0, 1])
            elif e < E - 1:
                w2_q = weights(loaded(w2_rows[e]), False, (e, PASSES) in VECTOR_CHUNKS)
                hidden_q.append(first_layer(e, w1_q))
                waiting = second_layer(e, hidden_q[e], w2_q, [0, 1, 2, 3])
            else:
                late = [half_of_w2(f, 1, False) for f in LATE]
                w2_q = [half_of_w2(e, h, h == 1) for h in range(2)]
                hidden_q.append(first_layer(e, w1_q))
        for f, w2_late in zip(LATE, late):
            for args in second_layer(f, hidden_q[f], w2_late, [2, 3]):
                scatter(*args)
        for h in range(2):
            for args in second_layer(E - 1, hidden_q[E - 1], w2_q[h], [2 * h, 2 * h + 1]):
                scatter(*args)

        for b in range(4):
            nc.sync.dma_start(out=out[b * P : (b + 1) * P, :], in_=windows[b][:])
